import numpy as np
CORES = [0,1,2,3]
N = 4
GROUPS = [[0,1],[2,3]]
def setup_inputs(rng):
    return {"x": rng.standard_normal((N, 128, 128), dtype=np.float32)}
def reference(x):
    y = np.empty((N, 128, 256), x.dtype)
    for g in GROUPS:
        s = np.concatenate([x[r] for r in g], axis=1)
        for r in g:
            y[r] = s
    return {"y": y}

SCRATCH = {
    "full": ("sbuf", [128, 256], "float32"),
}
SEMAPHORES = ["loaded", "sent", "arrived", "stored"]


def engines(mask):
    return bin(mask).count("1")


def rank_program(g, core, T, topo):
    rank = T.rank_of(core)
    if rank is None:
        return
    group = [m for m in T.tables["GROUPS"] if rank in m][0]
    pos = group.index(rank)
    width = T.x.shape[1]
    mine = T.full[:, pos * width:(pos + 1) * width]
    peers = [T.cores[r] for r in group if r != rank]

    g.sync.dma_start(mine, T.x[:]).then_inc(T.sem.loaded, 16)

    g.wait_ge(T.sem.loaded, 16)
    sent = 0
    for peer in peers:
        rid, pid, _ = topo.addr(peer)
        mask = topo.mask(core, peer)
        g.remote_dma(mine, mine, T.sem.arrived, T.sem.sent, pid, rid, mask)
        sent += engines(mask)

    arrived = sum(engines(topo.mask(peer, core)) for peer in peers)

    g.sync.wait_ge(T.sem.loaded, 16)
    g.sync.wait_ge(T.sem.arrived, arrived)
    g.sync.dma_start(T.y[:], T.full[:]).then_inc(T.sem.stored, 16)

    g.wait_ge(T.sem.sent, sent)
    g.wait_ge(T.sem.arrived, arrived)
    g.wait_ge(T.sem.stored, 16)
